import numpy as np
import ml_dtypes


def mxq(x, axis, fmt="e4m3"):
    dtype, down = {"e4m3": (ml_dtypes.float8_e4m3fn, 7), "e5m2": (ml_dtypes.float8_e5m2, 14)}[fmt]
    v = np.moveaxis(np.asarray(x, np.float32).astype(ml_dtypes.bfloat16).astype(np.float64), axis, -1)
    blocks = v.reshape(v.shape[:-1] + (-1, 32))
    amax = np.abs(blocks).max(-1, keepdims=True)
    byte = np.maximum(np.where(amax > 0, np.frexp(amax)[1] - 1 + 127, 0) - down, 1)
    scale = np.exp2(byte - 127.0)
    codes = (blocks / scale).astype(np.float32).astype(dtype).astype(np.float64)
    return np.moveaxis((codes * scale).reshape(v.shape), -1, axis)


WIDE = False


def mx_kscale(k):
    if not WIDE:
        return np.ones(k)
    levels = np.array([10, -10, 5, -5, 0])
    if k % 512:
        return np.exp2(np.random.permutation(np.resize(levels, k // 32))).repeat(32)
    a = np.empty((k // 512, 16))
    for p in range(k // 512):
        a[p, :8] = np.random.permutation(np.resize(levels, 8))
        for g in range(8):
            far = levels[np.abs(levels - a[p, g]) >= 10]
            a[p, g + 8] = far[np.random.randint(len(far))]
    return np.exp2(a.ravel()).repeat(32)


def f64(x):
    return np.asarray(x).astype(np.float64)


def striped(idx):
    return np.tile(np.asarray(idx).reshape(-1, 16).T, (8, 1)).astype(np.uint16)


def unstriped(offs):
    return offs[:16].T.reshape(-1).astype(np.int64)


G, T, T2, D, M = 512, 1024, 2048, 1536, 128


def setup_inputs():
    n = np.random.standard_normal
    s = mx_kscale(D)[:, None]
    return {
        "xT": (n((D, T)) * s).astype(np.float32),
        "w": (n((D, M)) / np.sqrt(D) / s).astype(np.float32),
        "cache": n((M, T2)).astype(np.float32),
        "offs": striped(np.random.permutation(T)[:G]),
        "slots": striped(np.random.permutation(T2)[:G]),
    }


def reference(xT, w, cache, offs, slots):
    y = mxq(f64(w), 0, "e4m3").T @ mxq(f64(xT)[:, unstriped(offs)], 0, "e4m3")
    out = f64(cache).copy()
    out[:, unstriped(slots)] = y
    return out

@@ -1,0 +1,151 @@
+from contextlib import ExitStack
+
+import concourse.mybir as mybir
+
+G, T, T2, D, M = 512, 1024, 2048, 1536, 128
+FLOPS = 2 * D * M * G
+
+F32 = mybir.dt.float32
+BF16 = mybir.dt.bfloat16
+U32 = mybir.dt.uint32
+U16 = mybir.dt.uint16
+U8 = mybir.dt.uint8
+FP8X4 = mybir.dt.float8_e4m3fn_x4
+COPY = mybir.ActivationFunctionType.Copy
+
+P = 128
+PACK = 4
+K_PASS = P * PACK
+PASSES = D // K_PASS
+HALF = G // 2
+LIST_HALF = HALF // 16
+V_COLS = 640
+
+
+def tile_attend_fill_kernel(tc, xT, w, cache, offs, slots, out):
+    nc = tc.nc
+    with ExitStack() as ctx:
+        keep = ctx.enter_context(tc.tile_pool(name="keep", bufs=1))
+        psum = ctx.enter_context(tc.psum_pool(name="psum", bufs=1))
+
+        offs_sb = keep.tile([P, G // 16], U16, name="offs_sb")
+        slots_sb = keep.tile([P, G // 16], U16, name="slots_sb")
+        window = keep.tile([P, T2], F32, name="window")
+        raw = [keep.tile([P, 2, T], F32, name="raw%d" % k) for k in range(2 * PASSES)]
+        pairs = [keep.tile([P, 2 * T], BF16, name="pairs%d" % k) for k in range(2 * PASSES)]
+        picked = [keep.tile([P, 2, G], U32, name="picked%d" % g) for g in range(PASSES)]
+        x_bf = [keep.tile([P, G * PACK], BF16, name="x_bf%d" % g, align_bytes=64) for g in range(PASSES)]
+        x_codes = [keep.tile([P, G], U32, name="x_codes%d" % g, align_bytes=64) for g in range(PASSES)]
+        x_scales = [keep.tile([P, G], U8, name="x_scales%d" % g, align_bytes=64) for g in range(PASSES)]
+        w_raw = [keep.tile([P, PACK, M], F32, name="w_raw%d" % g) for g in range(PASSES)]
+        w_bf = [keep.tile([P, M * PACK], BF16, name="w_bf%d" % g, align_bytes=64) for g in range(PASSES)]
+        w_codes = [keep.tile([P, M], U32, name="w_codes%d" % g, align_bytes=64) for g in range(PASSES)]
+        w_scales = [keep.tile([P, M], U8, name="w_scales%d" % g, align_bytes=64) for g in range(PASSES)]
+        y = keep.tile([P, G], F32, name="y")
+        warm_in = keep.tile([P, 8], F32, name="warm_in")
+        warm_out = keep.tile([P, 8], F32, name="warm_out")
+        acc = [psum.tile([P, HALF], F32, name="acc%d" % h) for h in range(2)]
+
+        def load_x(k):
+            g, u = divmod(k, 2)
+            rows = xT[g * K_PASS : (g + 1) * K_PASS, :].rearrange("(p j) n -> p j n", j=PACK)
+            nc.sync.dma_start(out=raw[k][:], in_=rows[:, 2 * u : 2 * u + 2, :])
+
+        load_x(0)
+        nc.sync.dma_start(offs_sb[:], offs)
+        nc.sync.dma_start(slots_sb[:], slots)
+        for k in range(1, 2 * PASSES):
+            load_x(k)
+        for g in range(PASSES):
+            rows = w[g * K_PASS : (g + 1) * K_PASS, :].rearrange("(p j) m -> p j m", j=PACK)
+            nc.sync.dma_start(out=w_raw[g][:], in_=rows)
+        nc.sync.dma_start(out=window[:], in_=cache)
+
+        nc.gpsimd.memset(warm_in[:], 0.0)
+        nc.scalar.activation(warm_out[:], warm_in[:], COPY)
+
+        def cast_x(k):
+            src = raw[k][:].rearrange("p e n -> p n e")
+            dst = pairs[k][:].rearrange("p (n e) -> p n e", e=2)
+            nc.vector.tensor_copy(dst[:, 0:V_COLS, :], src[:, 0:V_COLS, :])
+            nc.scalar.activation(dst[:, V_COLS:T, :], src[:, V_COLS:T, :], COPY)
+
+        def gather(k, c0, c1):
+            g, u = divmod(k, 2)
+            nc.vector.tensor_copy(
+                picked[g][:, u, c0:c1],
+                pairs[k][:].bitcast(U32).indirect(offs_sb[:, c0 // 16 : c1 // 16]),
+            )
+
+        def weave_scalar(g):
+            dst = x_bf[g][:].bitcast(U32).rearrange("p (n u) -> p n u", u=2)
+            nc.scalar.copy(dst, picked[g][:].rearrange("p u n -> p n u"))
+
+        def weave_vector(g, c0, c1):
+            src = picked[g][:].rearrange("p u n -> p (u n)").bitcast(BF16)
+            src = src.rearrange("p (u n e) -> p n u e", u=2, e=2)
+            dst = x_bf[g][:].rearrange("p (n u e) -> p n u e", u=2, e=2)
+            nc.vector.tensor_copy(dst[:, c0:c1], src[:, c0:c1])
+
+        def quant_x(g, c0, c1):
+            nc.vector.quantize_mx(
+                out=x_codes[g][:, c0:c1].bitcast(FP8X4),
+                scales=x_scales[g][:, c0:c1],
+                in_=x_bf[g][:, PACK * c0 : PACK * c1],
+            )
+
+        def cast_w(g):
+            dst = w_bf[g][:].rearrange("p (m j) -> p m j", j=PACK)
+            nc.scalar.activation(dst, w_raw[g][:].rearrange("p j m -> p m j"), COPY)
+
+        def quant_w(g):
+            nc.vector.quantize_mx(out=w_codes[g][:].bitcast(FP8X4), scales=w_scales[g][:], in_=w_bf[g][:])
+
+        def multiply(g, h):
+            cols = slice(h * HALF, (h + 1) * HALF)
+            nc.tensor.matmul_mx(
+                out=acc[h][:],
+                lhsT=w_codes[g][:].bitcast(FP8X4),
+                lhsT_scale=w_scales[g][:],
+                rhs=x_codes[g][:, cols].bitcast(FP8X4),
+                rhs_scale=x_scales[g][:, cols],
+                start=(g == 0),
+                stop=(g == PASSES - 1),
+            )
+
+        cast_x(0)
+        gather(0, 0, G)
+        cast_x(1)
+        gather(1, 0, G)
+        cast_x(2)
+        weave_scalar(0)
+        gather(2, 0, G)
+        cast_x(3)
+        quant_x(0, 0, G)
+        gather(3, 0, G)
+        cast_x(4)
+        weave_scalar(1)
+        gather(4, 0, G)
+        cast_x(5)
+        quant_x(1, 0, G)
+        for g in range(PASSES):
+            cast_w(g)
+        gather(5, 0, HALF)
+        gather(5, HALF, G)
+        weave_vector(2, 0, HALF)
+        quant_w(0)
+        quant_w(1)
+        quant_x(2, 0, HALF)
+        quant_w(2)
+        weave_vector(2, HALF, G)
+        quant_x(2, HALF, G)
+        for h in range(2):
+            for g in range(PASSES):
+                multiply(g, h)
+            nc.scalar.copy(y[:, h * HALF : (h + 1) * HALF], acc[h][:])
+        for h in range(2):
+            nc.vector.tensor_copy(
+                window[:].indirect(slots_sb[:, h * LIST_HALF : (h + 1) * LIST_HALF]),
+                y[:, h * HALF : (h + 1) * HALF],
+            )
+        nc.sync.dma_start(out=out, in_=window[:])

@@ -19,7 +19,7 @@ K_PASS = P * PACK
 PASSES = D // K_PASS
 HALF = G // 2
 LIST_HALF = HALF // 16
-V_COLS = 640
+SPLIT = [1, 1, 1, 2, 2, 2]
 
 
 def tile_attend_fill_kernel(tc, xT, w, cache, offs, slots, out):
@@ -31,7 +31,7 @@ def tile_attend_fill_kernel(tc, xT, w, cache, offs, slots, out):
         offs_sb = keep.tile([P, G // 16], U16, name="offs_sb")
         slots_sb = keep.tile([P, G // 16], U16, name="slots_sb")
         window = keep.tile([P, T2], F32, name="window")
-        raw = [keep.tile([P, 2, T], F32, name="raw%d" % k) for k in range(2 * PASSES)]
+        raw = {(k, h): keep.tile([P, 2, T // SPLIT[k]], F32, name="raw%d_%d" % (k, h)) for k in range(2 * PASSES) for h in range(SPLIT[k])}
         pairs = [keep.tile([P, 2 * T], BF16, name="pairs%d" % k) for k in range(2 * PASSES)]
         picked = [keep.tile([P, 2, G], U32, name="picked%d" % g) for g in range(PASSES)]
         x_bf = [keep.tile([P, G * PACK], BF16, name="x_bf%d" % g, align_bytes=64) for g in range(PASSES)]
@@ -46,40 +46,55 @@ def tile_attend_fill_kernel(tc, xT, w, cache, offs, slots, out):
         warm_out = keep.tile([P, 8], F32, name="warm_out")
         acc = [psum.tile([P, HALF], F32, name="acc%d" % h) for h in range(2)]
 
-        def load_x(k):
+        def load_x(k, h):
             g, u = divmod(k, 2)
+            wd = T // SPLIT[k]
             rows = xT[g * K_PASS : (g + 1) * K_PASS, :].rearrange("(p j) n -> p j n", j=PACK)
-            nc.sync.dma_start(out=raw[k][:], in_=rows[:, 2 * u : 2 * u + 2, :])
+            nc.sync.dma_start(out=raw[k, h][:], in_=rows[:, 2 * u : 2 * u + 2, h * wd : (h + 1) * wd])
 
-        load_x(0)
-        nc.sync.dma_start(offs_sb[:], offs)
-        nc.sync.dma_start(slots_sb[:], slots)
-        for k in range(1, 2 * PASSES):
-            load_x(k)
-        for g in range(PASSES):
+        def load_w(g):
             rows = w[g * K_PASS : (g + 1) * K_PASS, :].rearrange("(p j) m -> p j m", j=PACK)
             nc.sync.dma_start(out=w_raw[g][:], in_=rows)
+
+        load_x(0, 0)
+        nc.sync.dma_start(offs_sb[:], offs)
+        nc.sync.dma_start(slots_sb[:], slots)
+        load_x(1, 0)
+        load_x(2, 0)
+        load_x(3, 0)
+        load_x(3, 1)
+        load_x(4, 0)
+        load_x(4, 1)
+        load_x(5, 0)
+        load_x(5, 1)
+        load_w(0)
+        load_w(1)
+        load_w(2)
         nc.sync.dma_start(out=window[:], in_=cache)
 
         nc.gpsimd.memset(warm_in[:], 0.0)
         nc.scalar.activation(warm_out[:], warm_in[:], COPY)
 
-        def cast_x(k):
-            src = raw[k][:].rearrange("p e n -> p n e")
-            dst = pairs[k][:].rearrange("p (n e) -> p n e", e=2)
-            nc.vector.tensor_copy(dst[:, 0:V_COLS, :], src[:, 0:V_COLS, :])
-            nc.scalar.activation(dst[:, V_COLS:T, :], src[:, V_COLS:T, :], COPY)
+        def cast_x(k, h, c0, c1, on_vector):
+            n0 = h * (T // SPLIT[k])
+            src = raw[k, h][:].rearrange("p e n -> p n e")[:, c0:c1, :]
+            dst = pairs[k][:].rearrange("p (n e) -> p n e", e=2)[:, n0 + c0 : n0 + c1, :]
+            if on_vector:
+                nc.vector.tensor_copy(dst, src)
+            else:
+                nc.scalar.activation(dst, src, COPY)
 
-        def gather(k, c0, c1):
+        def gather(k, c0, c1, stepped):
             g, u = divmod(k, 2)
-            nc.vector.tensor_copy(
-                picked[g][:, u, c0:c1],
-                pairs[k][:].bitcast(U32).indirect(offs_sb[:, c0 // 16 : c1 // 16]),
-            )
+            if stepped:
+                dst = x_bf[g][:].bitcast(U32).rearrange("p (n u) -> p n u", u=2)[:, c0:c1, u]
+            else:
+                dst = picked[g][:, u, c0:c1]
+            nc.vector.tensor_copy(dst, pairs[k][:].bitcast(U32).indirect(offs_sb[:, c0 // 16 : c1 // 16]))
 
-        def weave_scalar(g):
+        def weave_scalar(g, c0, c1):
             dst = x_bf[g][:].bitcast(U32).rearrange("p (n u) -> p n u", u=2)
-            nc.scalar.copy(dst, picked[g][:].rearrange("p u n -> p n u"))
+            nc.scalar.copy(dst[:, c0:c1], picked[g][:].rearrange("p u n -> p n u")[:, c0:c1])
 
         def weave_vector(g, c0, c1):
             src = picked[g][:].rearrange("p u n -> p (u n)").bitcast(BF16)
@@ -94,9 +109,13 @@ def tile_attend_fill_kernel(tc, xT, w, cache, offs, slots, out):
                 in_=x_bf[g][:, PACK * c0 : PACK * c1],
             )
 
-        def cast_w(g):
+        def cast_w(g, on_vector):
             dst = w_bf[g][:].rearrange("p (m j) -> p m j", j=PACK)
-            nc.scalar.activation(dst, w_raw[g][:].rearrange("p j m -> p m j"), COPY)
+            src = w_raw[g][:].rearrange("p j m -> p m j")
+            if on_vector:
+                nc.vector.tensor_copy(dst, src)
+            else:
+                nc.scalar.activation(dst, src, COPY)
 
         def quant_w(g):
             nc.vector.quantize_mx(out=w_codes[g][:].bitcast(FP8X4), scales=w_scales[g][:], in_=w_bf[g][:])
@@ -113,39 +132,57 @@ def tile_attend_fill_kernel(tc, xT, w, cache, offs, slots, out):
                 stop=(g == PASSES - 1),
             )
 
-        cast_x(0)
-        gather(0, 0, G)
-        cast_x(1)
-        gather(1, 0, G)
-        cast_x(2)
-        weave_scalar(0)
-        gather(2, 0, G)
-        cast_x(3)
+        def drain(h):
+            nc.scalar.copy(y[:, h * HALF : (h + 1) * HALF], acc[h][:])
+
+        def scatter(h):
+            nc.vector.tensor_copy(
+                window[:].indirect(slots_sb[:, h * LIST_HALF : (h + 1) * LIST_HALF]),
+                y[:, h * HALF : (h + 1) * HALF],
+            )
+
+        cast_x(0, 0, 0, 640, True)
+        cast_x(0, 0, 640, 1024, False)
+        gather(0, 0, G, True)
+        cast_x(1, 0, 0, 640, True)
+        cast_x(1, 0, 640, 1024, False)
+        gather(1, 0, G, True)
+        cast_x(2, 0, 0, 128, True)
+        cast_x(2, 0, 128, 1024, False)
         quant_x(0, 0, G)
-        gather(3, 0, G)
-        cast_x(4)
-        weave_scalar(1)
-        gather(4, 0, G)
-        cast_x(5)
+        gather(2, 0, G, True)
+        cast_x(3, 0, 0, 256, True)
+        cast_x(3, 0, 256, 512, False)
+        cast_x(3, 1, 0, 512, False)
+        gather(3, 0, G, True)
+        cast_x(4, 0, 0, 96, True)
+        cast_x(4, 0, 96, 512, False)
+        cast_x(4, 1, 0, 512, False)
+        gather(4, 0, G, False)
+        cast_x(5, 0, 0, 512, False)
+        cast_x(5, 1, 0, 128, True)
+        cast_x(5, 1, 128, 512, False)
         quant_x(1, 0, G)
-        for g in range(PASSES):
-            cast_w(g)
-        gather(5, 0, HALF)
-        gather(5, HALF, G)
+        gather(5, 0, HALF, False)
+        gather(5, HALF, G, False)
+        cast_w(0, True)
+        cast_w(1, False)
+        cast_w(2, False)
         weave_vector(2, 0, HALF)
         quant_w(0)
         quant_w(1)
         quant_x(2, 0, HALF)
         quant_w(2)
-        weave_vector(2, HALF, G)
+        weave_scalar(2, HALF, G)
         quant_x(2, HALF, G)
-        for h in range(2):
-            for g in range(PASSES):
-                multiply(g, h)
-            nc.scalar.copy(y[:, h * HALF : (h + 1) * HALF], acc[h][:])
-        for h in range(2):
-            nc.vector.tensor_copy(
-                window[:].indirect(slots_sb[:, h * LIST_HALF : (h + 1) * LIST_HALF]),
-                y[:, h * HALF : (h + 1) * HALF],
-            )
+        multiply(0, 0)
+        multiply(1, 0)
+        multiply(2, 0)
+        drain(0)
+        multiply(0, 1)
+        multiply(1, 1)
+        multiply(2, 1)
+        drain(1)
+        scatter(0)
+        scatter(1)
         nc.sync.dma_start(out=out, in_=window[:])

@@ -19,7 +19,7 @@ K_PASS = P * PACK
 PASSES = D // K_PASS
 HALF = G // 2
 LIST_HALF = HALF // 16
-SPLIT = [1, 1, 1, 2, 2, 2]
+SPLIT = [1, 1, 1, 1, 2, 2]
 
 
 def tile_attend_fill_kernel(tc, xT, w, cache, offs, slots, out):
@@ -58,11 +58,9 @@ def tile_attend_fill_kernel(tc, xT, w, cache, offs, slots, out):
 
         load_x(0, 0)
         nc.sync.dma_start(offs_sb[:], offs)
-        nc.sync.dma_start(slots_sb[:], slots)
         load_x(1, 0)
         load_x(2, 0)
         load_x(3, 0)
-        load_x(3, 1)
         load_x(4, 0)
         load_x(4, 1)
         load_x(5, 0)
@@ -70,6 +68,7 @@ def tile_attend_fill_kernel(tc, xT, w, cache, offs, slots, out):
         load_w(0)
         load_w(1)
         load_w(2)
+        nc.sync.dma_start(slots_sb[:], slots)
         nc.sync.dma_start(out=window[:], in_=cache)
 
         nc.gpsimd.memset(warm_in[:], 0.0)
@@ -109,9 +108,9 @@ def tile_attend_fill_kernel(tc, xT, w, cache, offs, slots, out):
                 in_=x_bf[g][:, PACK * c0 : PACK * c1],
             )
 
-        def cast_w(g, on_vector):
-            dst = w_bf[g][:].rearrange("p (m j) -> p m j", j=PACK)
-            src = w_raw[g][:].rearrange("p j m -> p m j")
+        def cast_w(g, m0, m1, on_vector):
+            dst = w_bf[g][:, PACK * m0 : PACK * m1].rearrange("p (c i j) -> p c j i", i=4, j=PACK)
+            src = w_raw[g][:, :, m0:m1].rearrange("p j (c i) -> p c j i", i=4)
             if on_vector:
                 nc.vector.tensor_copy(dst, src)
             else:
@@ -143,34 +142,36 @@ def tile_attend_fill_kernel(tc, xT, w, cache, offs, slots, out):
 
         cast_x(0, 0, 0, 640, True)
         cast_x(0, 0, 640, 1024, False)
-        gather(0, 0, G, True)
-        cast_x(1, 0, 0, 640, True)
-        cast_x(1, 0, 640, 1024, False)
-        gather(1, 0, G, True)
-        cast_x(2, 0, 0, 128, True)
-        cast_x(2, 0, 128, 1024, False)
+        gather(0, 0, G, False)
+        cast_x(1, 0, 0, 448, True)
+        cast_x(1, 0, 448, 1024, False)
+        gather(1, 0, G, False)
+        cast_x(2, 0, 0, 224, True)
+        cast_x(2, 0, 224, 1024, False)
+        weave_vector(0, 0, G)
+        gather(2, 0, G, False)
         quant_x(0, 0, G)
-        gather(2, 0, G, True)
-        cast_x(3, 0, 0, 256, True)
-        cast_x(3, 0, 256, 512, False)
-        cast_x(3, 1, 0, 512, False)
-        gather(3, 0, G, True)
-        cast_x(4, 0, 0, 96, True)
-        cast_x(4, 0, 96, 512, False)
-        cast_x(4, 1, 0, 512, False)
+        cast_x(3, 0, 0, 192, True)
+        cast_x(3, 0, 192, 1024, False)
+        gather(3, 0, G, False)
+        cast_x(4, 0, 0, 288, True)
+        cast_x(4, 0, 288, 512, False)
+        cast_x(4, 1, 0, 160, True)
+        cast_x(4, 1, 160, 512, False)
+        weave_vector(1, 0, G)
         gather(4, 0, G, False)
         cast_x(5, 0, 0, 512, False)
-        cast_x(5, 1, 0, 128, True)
-        cast_x(5, 1, 128, 512, False)
+        cast_x(5, 1, 0, 512, False)
         quant_x(1, 0, G)
+        cast_w(0, 0, M, False)
         gather(5, 0, HALF, False)
-        gather(5, HALF, G, False)
-        cast_w(0, True)
-        cast_w(1, False)
-        cast_w(2, False)
-        weave_vector(2, 0, HALF)
         quant_w(0)
+        gather(5, HALF, G, False)
+        cast_w(1, 0, M, False)
+        weave_scalar(2, 0, HALF)
         quant_w(1)
+        cast_w(2, 0, 80, True)
+        cast_w(2, 80, M, False)
         quant_x(2, 0, HALF)
         quant_w(2)
         weave_scalar(2, HALF, G)

@@ -19,6 +19,7 @@ K_PASS = P * PACK
 PASSES = D // K_PASS
 HALF = G // 2
 LIST_HALF = HALF // 16
+PIECES = [(0, 128), (128, 256), (256, 512)]
 SPLIT = [1, 1, 1, 1, 2, 2]
 
 
@@ -31,7 +32,7 @@ def tile_attend_fill_kernel(tc, xT, w, cache, offs, slots, out):
         offs_sb = keep.tile([P, G // 16], U16, name="offs_sb")
         slots_sb = keep.tile([P, G // 16], U16, name="slots_sb")
         window = keep.tile([P, T2], F32, name="window")
-        raw = {(k, h): keep.tile([P, 2, T // SPLIT[k]], F32, name="raw%d_%d" % (k, h)) for k in range(2 * PASSES) for h in range(SPLIT[k])}
+        raw = {(k, h): keep.tile([P, 2, T // SPLIT[k]], F32, name="raw%d_%d" % (k, h), align_bytes=64) for k in range(2 * PASSES) for h in range(SPLIT[k])}
         pairs = [keep.tile([P, 2 * T], BF16, name="pairs%d" % k) for k in range(2 * PASSES)]
         picked = [keep.tile([P, 2, G], U32, name="picked%d" % g) for g in range(PASSES)]
         x_bf = [keep.tile([P, G * PACK], BF16, name="x_bf%d" % g, align_bytes=64) for g in range(PASSES)]
@@ -44,7 +45,7 @@ def tile_attend_fill_kernel(tc, xT, w, cache, offs, slots, out):
         y = keep.tile([P, G], F32, name="y")
         warm_in = keep.tile([P, 8], F32, name="warm_in")
         warm_out = keep.tile([P, 8], F32, name="warm_out")
-        acc = [psum.tile([P, HALF], F32, name="acc%d" % h) for h in range(2)]
+        acc = [psum.tile([P, c1 - c0], F32, name="acc%d" % c0) for c0, c1 in PIECES]
 
         def load_x(k, h):
             g, u = divmod(k, 2)
@@ -63,9 +64,9 @@ def tile_attend_fill_kernel(tc, xT, w, cache, offs, slots, out):
         load_x(3, 0)
         load_x(4, 0)
         load_x(4, 1)
+        load_w(0)
         load_x(5, 0)
         load_x(5, 1)
-        load_w(0)
         load_w(1)
         load_w(2)
         nc.sync.dma_start(slots_sb[:], slots)
@@ -120,7 +121,7 @@ def tile_attend_fill_kernel(tc, xT, w, cache, offs, slots, out):
             nc.vector.quantize_mx(out=w_codes[g][:].bitcast(FP8X4), scales=w_scales[g][:], in_=w_bf[g][:])
 
         def multiply(g, h):
-            cols = slice(h * HALF, (h + 1) * HALF)
+            cols = slice(PIECES[h][0], PIECES[h][1])
             nc.tensor.matmul_mx(
                 out=acc[h][:],
                 lhsT=w_codes[g][:].bitcast(FP8X4),
@@ -132,7 +133,7 @@ def tile_attend_fill_kernel(tc, xT, w, cache, offs, slots, out):
             )
 
         def drain(h):
-            nc.scalar.copy(y[:, h * HALF : (h + 1) * HALF], acc[h][:])
+            nc.scalar.copy(y[:, PIECES[h][0] : PIECES[h][1]], acc[h][:])
 
         def scatter(h):
             nc.vector.tensor_copy(
@@ -146,44 +147,54 @@ def tile_attend_fill_kernel(tc, xT, w, cache, offs, slots, out):
         cast_x(1, 0, 0, 448, True)
         cast_x(1, 0, 448, 1024, False)
         gather(1, 0, G, False)
-        cast_x(2, 0, 0, 224, True)
-        cast_x(2, 0, 224, 1024, False)
         weave_vector(0, 0, G)
-        gather(2, 0, G, False)
+        cast_x(2, 0, 0, 192, True)
+        cast_x(2, 0, 192, 1024, False)
         quant_x(0, 0, G)
+        gather(2, 0, G, False)
         cast_x(3, 0, 0, 192, True)
         cast_x(3, 0, 192, 1024, False)
-        gather(3, 0, G, False)
         cast_x(4, 0, 0, 288, True)
         cast_x(4, 0, 288, 512, False)
-        cast_x(4, 1, 0, 160, True)
-        cast_x(4, 1, 160, 512, False)
-        weave_vector(1, 0, G)
+        gather(3, 0, G, False)
+        cast_x(4, 1, 0, 32, True)
+        cast_x(4, 1, 32, 512, False)
+        cast_w(0, 0, 80, True)
+        cast_w(0, 80, M, False)
+        x_bf[1] = keep.tile([P, G * PACK], BF16, name="late_x_bf1", tag="raw4_1", align_bytes=64)
+        weave_vector(1, 0, HALF)
+        weave_scalar(1, HALF, G)
         gather(4, 0, G, False)
-        cast_x(5, 0, 0, 512, False)
-        cast_x(5, 1, 0, 512, False)
-        quant_x(1, 0, G)
-        cast_w(0, 0, M, False)
-        gather(5, 0, HALF, False)
         quant_w(0)
-        gather(5, HALF, G, False)
-        cast_w(1, 0, M, False)
-        weave_scalar(2, 0, HALF)
+        cast_x(5, 0, 0, 512, False)
+        quant_x(1, 0, G)
+        cast_x(5, 1, 0, 128, True)
+        cast_x(5, 1, 128, 512, False)
+        cast_w(1, 0, 128, True)
+        cast_w(2, 0, M, False)
+        gather(5, 0, 128, False)
+        gather(5, 128, 256, False)
         quant_w(1)
-        cast_w(2, 0, 80, True)
-        cast_w(2, 80, M, False)
-        quant_x(2, 0, HALF)
+        weave_scalar(2, 0, 128)
+        weave_scalar(2, 128, 256)
         quant_w(2)
-        weave_scalar(2, HALF, G)
-        quant_x(2, HALF, G)
+        quant_x(2, 0, 128)
+        quant_x(2, 128, 256)
+        gather(5, 256, 512, False)
         multiply(0, 0)
+        multiply(0, 1)
         multiply(1, 0)
+        multiply(1, 1)
         multiply(2, 0)
         drain(0)
-        multiply(0, 1)
-        multiply(1, 1)
         multiply(2, 1)
         drain(1)
+        weave_scalar(2, 256, 512)
+        quant_x(2, 256, 512)
+        multiply(0, 2)
+        multiply(1, 2)
+        multiply(2, 2)
+        drain(2)
         scatter(0)
         scatter(1)
         nc.sync.dma_start(out=out, in_=window[:])

@@ -12,15 +12,19 @@ U16 = mybir.dt.uint16
 U8 = mybir.dt.uint8
 FP8X4 = mybir.dt.float8_e4m3fn_x4
 COPY = mybir.ActivationFunctionType.Copy
+MULT = mybir.AluOpType.mult
+ADD = mybir.AluOpType.add
 
 P = 128
 PACK = 4
 K_PASS = P * PACK
 PASSES = D // K_PASS
+PAIRS = 2 * PASSES
 HALF = G // 2
-LIST_HALF = HALF // 16
+LAST = PASSES - 1
+VECTOR_COLUMNS = [672, 672, 640, 192, 160, 336]
+LOADS = [1, 1, 1, 2, 2, 2]
 PIECES = [(0, 128), (128, 256), (256, 512)]
-SPLIT = [1, 1, 1, 1, 2, 2]
 
 
 def tile_attend_fill_kernel(tc, xT, w, cache, offs, slots, out):
@@ -32,104 +36,108 @@ def tile_attend_fill_kernel(tc, xT, w, cache, offs, slots, out):
         offs_sb = keep.tile([P, G // 16], U16, name="offs_sb")
         slots_sb = keep.tile([P, G // 16], U16, name="slots_sb")
         window = keep.tile([P, T2], F32, name="window")
-        raw = {(k, h): keep.tile([P, 2, T // SPLIT[k]], F32, name="raw%d_%d" % (k, h), align_bytes=64) for k in range(2 * PASSES) for h in range(SPLIT[k])}
-        pairs = [keep.tile([P, 2 * T], BF16, name="pairs%d" % k) for k in range(2 * PASSES)]
-        picked = [keep.tile([P, 2, G], U32, name="picked%d" % g) for g in range(PASSES)]
-        x_bf = [keep.tile([P, G * PACK], BF16, name="x_bf%d" % g, align_bytes=64) for g in range(PASSES)]
-        x_codes = [keep.tile([P, G], U32, name="x_codes%d" % g, align_bytes=64) for g in range(PASSES)]
-        x_scales = [keep.tile([P, G], U8, name="x_scales%d" % g, align_bytes=64) for g in range(PASSES)]
-        w_raw = [keep.tile([P, PACK, M], F32, name="w_raw%d" % g) for g in range(PASSES)]
-        w_bf = [keep.tile([P, M * PACK], BF16, name="w_bf%d" % g, align_bytes=64) for g in range(PASSES)]
+        raw = {
+            (k, i): keep.tile([P, 2, T // LOADS[k]], F32, name="raw%d_%d" % (k, i), align_bytes=64)
+            for k in range(PAIRS)
+            for i in range(LOADS[k])
+        }
+        pairs = [keep.tile([P, 2 * T], BF16, name="pairs%d" % k) for k in range(PAIRS)]
+        picked = {(g, 0): keep.tile([P, 2, G], U32, name="picked%d" % g) for g in range(LAST)}
+        for h in range(2):
+            picked.setdefault((LAST, h * HALF), keep.tile([P, 2, HALF], U32, name="picked_last%d" % h, align_bytes=64))
+        w_raw = [keep.tile([P, PACK, M], F32, name="w_raw%d" % g, align_bytes=64) for g in range(PASSES)]
         w_codes = [keep.tile([P, M], U32, name="w_codes%d" % g, align_bytes=64) for g in range(PASSES)]
         w_scales = [keep.tile([P, M], U8, name="w_scales%d" % g, align_bytes=64) for g in range(PASSES)]
+        x_scales = [keep.tile([P, G], U8, name="x_scales%d" % g, align_bytes=64) for g in range(PASSES)]
         y = keep.tile([P, G], F32, name="y")
         warm_in = keep.tile([P, 8], F32, name="warm_in")
         warm_out = keep.tile([P, 8], F32, name="warm_out")
         acc = [psum.tile([P, c1 - c0], F32, name="acc%d" % c0) for c0, c1 in PIECES]
+        x_bf = {}
+        w_bf = {}
+        x_codes = {}
 
-        def load_x(k, h):
+        def load_x(k):
             g, u = divmod(k, 2)
-            wd = T // SPLIT[k]
             rows = xT[g * K_PASS : (g + 1) * K_PASS, :].rearrange("(p j) n -> p j n", j=PACK)
-            nc.sync.dma_start(out=raw[k, h][:], in_=rows[:, 2 * u : 2 * u + 2, h * wd : (h + 1) * wd])
+            width = T // LOADS[k]
+            for i in range(LOADS[k]):
+                nc.sync.dma_start(out=raw[k, i][:], in_=rows[:, 2 * u : 2 * u + 2, i * width : (i + 1) * width])
 
         def load_w(g):
             rows = w[g * K_PASS : (g + 1) * K_PASS, :].rearrange("(p j) m -> p j m", j=PACK)
             nc.sync.dma_start(out=w_raw[g][:], in_=rows)
 
-        load_x(0, 0)
+        load_x(0)
         nc.sync.dma_start(offs_sb[:], offs)
-        load_x(1, 0)
-        load_x(2, 0)
-        load_x(3, 0)
-        load_x(4, 0)
-        load_x(4, 1)
+        for k in range(1, PAIRS - 1):
+            load_x(k)
         load_w(0)
-        load_x(5, 0)
-        load_x(5, 1)
-        load_w(1)
-        load_w(2)
+        load_x(PAIRS - 1)
+        for g in range(1, PASSES):
+            load_w(g)
         nc.sync.dma_start(slots_sb[:], slots)
         nc.sync.dma_start(out=window[:], in_=cache)
 
         nc.gpsimd.memset(warm_in[:], 0.0)
         nc.scalar.activation(warm_out[:], warm_in[:], COPY)
 
-        def cast_x(k, h, c0, c1, on_vector):
-            n0 = h * (T // SPLIT[k])
-            src = raw[k, h][:].rearrange("p e n -> p n e")[:, c0:c1, :]
-            dst = pairs[k][:].rearrange("p (n e) -> p n e", e=2)[:, n0 + c0 : n0 + c1, :]
-            if on_vector:
-                nc.vector.tensor_copy(dst, src)
-            else:
-                nc.scalar.activation(dst, src, COPY)
+        def cast_x(k):
+            width = T // LOADS[k]
+            for i in range(LOADS[k]):
+                cut = VECTOR_COLUMNS[k] if i == LOADS[k] - 1 else 0
+                src = raw[k, i][:].rearrange("p e n -> p n e")
+                dst = pairs[k][:].rearrange("p (n e) -> p n e", e=2)[:, i * width : (i + 1) * width, :]
+                if cut:
+                    nc.vector.tensor_copy(dst[:, :cut, :], src[:, :cut, :])
+                nc.scalar.activation(dst[:, cut:, :], src[:, cut:, :], COPY)
 
-        def gather(k, c0, c1, stepped):
+        def gather(k, c0, c1):
             g, u = divmod(k, 2)
-            if stepped:
-                dst = x_bf[g][:].bitcast(U32).rearrange("p (n u) -> p n u", u=2)[:, c0:c1, u]
-            else:
-                dst = picked[g][:, u, c0:c1]
-            nc.vector.tensor_copy(dst, pairs[k][:].bitcast(U32).indirect(offs_sb[:, c0 // 16 : c1 // 16]))
+            base = c0 - c0 % HALF if g == LAST else 0
+            nc.vector.tensor_copy(picked[g, base][:, u, c0 - base : c1 - base], pairs[k][:].bitcast(U32).indirect(offs_sb[:, c0 // 16 : c1 // 16]))
 
-        def weave_scalar(g, c0, c1):
-            dst = x_bf[g][:].bitcast(U32).rearrange("p (n u) -> p n u", u=2)
-            nc.scalar.copy(dst[:, c0:c1], picked[g][:].rearrange("p u n -> p n u")[:, c0:c1])
+        def new_input(g, h, tag):
+            x_bf[g, h] = keep.tile([P, HALF * PACK], BF16, name="x_bf%d_%d" % (g, h), tag=tag, align_bytes=64)
 
-        def weave_vector(g, c0, c1):
-            src = picked[g][:].rearrange("p u n -> p (u n)").bitcast(BF16)
-            src = src.rearrange("p (u n e) -> p n u e", u=2, e=2)
-            dst = x_bf[g][:].rearrange("p (n u e) -> p n u e", u=2, e=2)
-            nc.vector.tensor_copy(dst[:, c0:c1], src[:, c0:c1])
+        def new_codes(g, h, tag):
+            x_codes[g, h] = keep.tile([P, HALF], U32, name="x_codes%d_%d" % (g, h), tag=tag, align_bytes=64)
+
+        def weave(copy, g, c0, c1):
+            h, first = c0 // HALF, c0 % HALF
+            dst = x_bf[g, h][:].bitcast(U32).rearrange("p (n u) -> p n u", u=2)
+            base = c0 - c0 % HALF if g == LAST else 0
+            copy(dst[:, first : first + c1 - c0], picked[g, base][:].rearrange("p u n -> p n u")[:, c0 - base : c1 - base])
 
         def quant_x(g, c0, c1):
+            h, first = c0 // HALF, c0 % HALF
+            last = first + c1 - c0
             nc.vector.quantize_mx(
-                out=x_codes[g][:, c0:c1].bitcast(FP8X4),
+                out=x_codes[g, h][:, first:last].bitcast(FP8X4),
                 scales=x_scales[g][:, c0:c1],
-                in_=x_bf[g][:, PACK * c0 : PACK * c1],
+                in_=x_bf[g, h][:, PACK * first : PACK * last],
             )
 
-        def cast_w(g, m0, m1, on_vector):
-            dst = w_bf[g][:, PACK * m0 : PACK * m1].rearrange("p (c i j) -> p c j i", i=4, j=PACK)
-            src = w_raw[g][:, :, m0:m1].rearrange("p j (c i) -> p c j i", i=4)
-            if on_vector:
-                nc.vector.tensor_copy(dst, src)
-            else:
-                nc.scalar.activation(dst, src, COPY)
+        def cast_w_scalar(g, tag):
+            w_bf[g] = keep.tile([P, M * PACK], BF16, name="w_bf%d" % g, tag=tag, align_bytes=64)
+            dst = w_bf[g][:].rearrange("p (c i j) -> p c j i", i=4, j=PACK)
+            src = w_raw[g][:].rearrange("p j (c i) -> p c j i", i=4)
+            nc.scalar.activation(dst, src, COPY)
 
         def quant_w(g):
             nc.vector.quantize_mx(out=w_codes[g][:].bitcast(FP8X4), scales=w_scales[g][:], in_=w_bf[g][:])
 
         def multiply(g, h):
-            cols = slice(PIECES[h][0], PIECES[h][1])
+            c0, c1 = PIECES[h]
+            first = c0 - c0 % HALF
             nc.tensor.matmul_mx(
                 out=acc[h][:],
                 lhsT=w_codes[g][:].bitcast(FP8X4),
                 lhsT_scale=w_scales[g][:],
-                rhs=x_codes[g][:, cols].bitcast(FP8X4),
-                rhs_scale=x_scales[g][:, cols],
+                rhs=x_codes[g, c0 // HALF][:, c0 - first : c1 - first].bitcast(FP8X4),
+                rhs_scale=x_scales[g][:, c0:c1],
                 start=(g == 0),
-                stop=(g == PASSES - 1),
+                stop=(g == LAST),
             )
 
         def drain(h):
@@ -137,64 +145,48 @@ def tile_attend_fill_kernel(tc, xT, w, cache, offs, slots, out):
 
         def scatter(h):
             nc.vector.tensor_copy(
-                window[:].indirect(slots_sb[:, h * LIST_HALF : (h + 1) * LIST_HALF]),
+                window[:].indirect(slots_sb[:, h * HALF // 16 : (h + 1) * HALF // 16]),
                 y[:, h * HALF : (h + 1) * HALF],
             )
 
-        cast_x(0, 0, 0, 640, True)
-        cast_x(0, 0, 640, 1024, False)
-        gather(0, 0, G, False)
-        cast_x(1, 0, 0, 448, True)
-        cast_x(1, 0, 448, 1024, False)
-        gather(1, 0, G, False)
-        weave_vector(0, 0, G)
-        cast_x(2, 0, 0, 192, True)
-        cast_x(2, 0, 192, 1024, False)
-        quant_x(0, 0, G)
-        gather(2, 0, G, False)
-        cast_x(3, 0, 0, 192, True)
-        cast_x(3, 0, 192, 1024, False)
-        cast_x(4, 0, 0, 288, True)
-        cast_x(4, 0, 288, 512, False)
-        gather(3, 0, G, False)
-        cast_x(4, 1, 0, 32, True)
-        cast_x(4, 1, 32, 512, False)
-        cast_w(0, 0, 80, True)
-        cast_w(0, 80, M, False)
-        x_bf[1] = keep.tile([P, G * PACK], BF16, name="late_x_bf1", tag="raw4_1", align_bytes=64)
-        weave_vector(1, 0, HALF)
-        weave_scalar(1, HALF, G)
-        gather(4, 0, G, False)
+        for k in range(PAIRS - 1):
+            cast_x(k)
+            if k // 2 == LAST:
+                gather(k, 0, HALF)
+                gather(k, HALF, G)
+            else:
+                gather(k, 0, G)
+            if k >= 2:
+                g, h = divmod(k - 2, 2)
+                new_input(g, h, "raw%d_%d" % (k, LOADS[k] - 1))
+                weave(nc.gpsimd.tensor_copy, g, h * HALF, (h + 1) * HALF)
+                new_codes(g, h, "x_codes%d_%d" % (g, h))
+                quant_x(g, h * HALF, (h + 1) * HALF)
+        cast_w_scalar(0, "w_bf0")
         quant_w(0)
-        cast_x(5, 0, 0, 512, False)
-        quant_x(1, 0, G)
-        cast_x(5, 1, 0, 128, True)
-        cast_x(5, 1, 128, 512, False)
-        cast_w(1, 0, 128, True)
-        cast_w(2, 0, M, False)
-        gather(5, 0, 128, False)
-        gather(5, 128, 256, False)
-        quant_w(1)
-        weave_scalar(2, 0, 128)
-        weave_scalar(2, 128, 256)
-        quant_w(2)
-        quant_x(2, 0, 128)
-        quant_x(2, 128, 256)
-        gather(5, 256, 512, False)
-        multiply(0, 0)
-        multiply(0, 1)
-        multiply(1, 0)
-        multiply(1, 1)
-        multiply(2, 0)
-        drain(0)
-        multiply(2, 1)
-        drain(1)
-        weave_scalar(2, 256, 512)
-        quant_x(2, 256, 512)
-        multiply(0, 2)
-        multiply(1, 2)
-        multiply(2, 2)
-        drain(2)
+        cast_x(PAIRS - 1)
+        new_input(1, 1, "raw5_1")
+        weave(nc.gpsimd.tensor_copy, 1, HALF, G)
+        for c0, c1 in PIECES:
+            gather(PAIRS - 1, c0, c1)
+        for g in range(1, PASSES):
+            cast_w_scalar(g, "w_bf%d" % g)
+            quant_w(g)
+        new_input(LAST, 0, "w_raw2")
+        new_codes(LAST, 0, "x_codes2_0")
+        for c0, c1 in PIECES[:2]:
+            weave(nc.scalar.copy, LAST, c0, c1)
+            quant_x(LAST, c0, c1)
+        new_input(LAST, 1, "picked_last0")
+        weave(nc.scalar.copy, LAST, HALF, G)
+        new_codes(1, 1, "w_raw2")
+        quant_x(1, HALF, G)
+        new_codes(LAST, 1, "x_codes2_1")
+        quant_x(LAST, HALF, G)
+        for h in range(len(PIECES)):
+            for g in range(PASSES):
+                multiply(g, h)
+            drain(h)
         scatter(0)
         scatter(1)
         nc.sync.dma_start(out=out, in_=window[:])

@@ -22,8 +22,8 @@ PASSES = D // K_PASS
 PAIRS = 2 * PASSES
 HALF = G // 2
 LAST = PASSES - 1
-VECTOR_COLUMNS = [672, 672, 640, 192, 160, 336]
-LOADS = [1, 1, 1, 2, 2, 2]
+VECTOR_COLUMNS = [672, 672, 640, 288, 256, 400]
+EARLY = [0, 0, 0, 384, 384, 384]
 PIECES = [(0, 128), (128, 256), (256, 512)]
 
 
@@ -36,11 +36,7 @@ def tile_attend_fill_kernel(tc, xT, w, cache, offs, slots, out):
         offs_sb = keep.tile([P, G // 16], U16, name="offs_sb")
         slots_sb = keep.tile([P, G // 16], U16, name="slots_sb")
         window = keep.tile([P, T2], F32, name="window")
-        raw = {
-            (k, i): keep.tile([P, 2, T // LOADS[k]], F32, name="raw%d_%d" % (k, i), align_bytes=64)
-            for k in range(PAIRS)
-            for i in range(LOADS[k])
-        }
+        raw = [keep.tile([P, 2 * T], F32, name="raw%d" % k, align_bytes=64) for k in range(PAIRS)]
         pairs = [keep.tile([P, 2 * T], BF16, name="pairs%d" % k) for k in range(PAIRS)]
         picked = {(g, 0): keep.tile([P, 2, G], U32, name="picked%d" % g) for g in range(LAST)}
         for h in range(2):
@@ -59,10 +55,11 @@ def tile_attend_fill_kernel(tc, xT, w, cache, offs, slots, out):
 
         def load_x(k):
             g, u = divmod(k, 2)
-            rows = xT[g * K_PASS : (g + 1) * K_PASS, :].rearrange("(p j) n -> p j n", j=PACK)
-            width = T // LOADS[k]
-            for i in range(LOADS[k]):
-                nc.sync.dma_start(out=raw[k, i][:], in_=rows[:, 2 * u : 2 * u + 2, i * width : (i + 1) * width])
+            rows = xT[g * K_PASS : (g + 1) * K_PASS, :].rearrange("(p u e) n -> p u (e n)", u=2, e=2)[:, u, :]
+            cut = T + EARLY[k] if EARLY[k] else 2 * T
+            nc.sync.dma_start(out=raw[k][:, :cut], in_=rows[:, :cut])
+            if EARLY[k]:
+                nc.sync.dma_start(out=raw[k][:, cut:], in_=rows[:, cut:])
 
         def load_w(g):
             rows = w[g * K_PASS : (g + 1) * K_PASS, :].rearrange("(p j) m -> p j m", j=PACK)
@@ -83,14 +80,13 @@ def tile_attend_fill_kernel(tc, xT, w, cache, offs, slots, out):
         nc.scalar.activation(warm_out[:], warm_in[:], COPY)
 
         def cast_x(k):
-            width = T // LOADS[k]
-            for i in range(LOADS[k]):
-                cut = VECTOR_COLUMNS[k] if i == LOADS[k] - 1 else 0
-                src = raw[k, i][:].rearrange("p e n -> p n e")
-                dst = pairs[k][:].rearrange("p (n e) -> p n e", e=2)[:, i * width : (i + 1) * width, :]
-                if cut:
-                    nc.vector.tensor_copy(dst[:, :cut, :], src[:, :cut, :])
-                nc.scalar.activation(dst[:, cut:, :], src[:, cut:, :], COPY)
+            src = raw[k][:].rearrange("p (e n) -> p n e", e=2)
+            dst = pairs[k][:].rearrange("p (n e) -> p n e", e=2)
+            early, cut = EARLY[k], T - VECTOR_COLUMNS[k]
+            if early:
+                nc.scalar.activation(dst[:, :early, :], src[:, :early, :], COPY)
+            nc.vector.tensor_copy(dst[:, cut:, :], src[:, cut:, :])
+            nc.scalar.activation(dst[:, early:cut, :], src[:, early:cut, :], COPY)
 
         def gather(k, c0, c1):
             g, u = divmod(k, 2)
@@ -158,14 +154,14 @@ def tile_attend_fill_kernel(tc, xT, w, cache, offs, slots, out):
                 gather(k, 0, G)
             if k >= 2:
                 g, h = divmod(k - 2, 2)
-                new_input(g, h, "raw%d_%d" % (k, LOADS[k] - 1))
+                new_input(g, h, "raw%d" % k)
                 weave(nc.gpsimd.tensor_copy, g, h * HALF, (h + 1) * HALF)
                 new_codes(g, h, "x_codes%d_%d" % (g, h))
                 quant_x(g, h * HALF, (h + 1) * HALF)
         cast_w_scalar(0, "w_bf0")
         quant_w(0)
         cast_x(PAIRS - 1)
-        new_input(1, 1, "raw5_1")
+        new_input(1, 1, "raw5")
         weave(nc.gpsimd.tensor_copy, 1, HALF, G)
         for c0, c1 in PIECES:
             gather(PAIRS - 1, c0, c1)

@@ -22,7 +22,7 @@ PASSES = D // K_PASS
 PAIRS = 2 * PASSES
 HALF = G // 2
 LAST = PASSES - 1
-VECTOR_COLUMNS = [672, 672, 640, 288, 256, 400]
+VECTOR_COLUMNS = [672, 672, 640, 288, 352, 400]
 EARLY = [0, 0, 0, 384, 384, 384]
 PIECES = [(0, 128), (128, 256), (256, 512)]
 
@@ -39,8 +39,8 @@ def tile_attend_fill_kernel(tc, xT, w, cache, offs, slots, out):
         raw = [keep.tile([P, 2 * T], F32, name="raw%d" % k, align_bytes=64) for k in range(PAIRS)]
         pairs = [keep.tile([P, 2 * T], BF16, name="pairs%d" % k) for k in range(PAIRS)]
         picked = {(g, 0): keep.tile([P, 2, G], U32, name="picked%d" % g) for g in range(LAST)}
-        for h in range(2):
-            picked.setdefault((LAST, h * HALF), keep.tile([P, 2, HALF], U32, name="picked_last%d" % h, align_bytes=64))
+        for c0, c1 in PIECES:
+            picked.setdefault((LAST, c0), keep.tile([P, 2, c1 - c0], U32, name="picked_last%d" % c0, align_bytes=64))
         w_raw = [keep.tile([P, PACK, M], F32, name="w_raw%d" % g, align_bytes=64) for g in range(PASSES)]
         w_codes = [keep.tile([P, M], U32, name="w_codes%d" % g, align_bytes=64) for g in range(PASSES)]
         w_scales = [keep.tile([P, M], U8, name="w_scales%d" % g, align_bytes=64) for g in range(PASSES)]
@@ -90,7 +90,7 @@ def tile_attend_fill_kernel(tc, xT, w, cache, offs, slots, out):
 
         def gather(k, c0, c1):
             g, u = divmod(k, 2)
-            base = c0 - c0 % HALF if g == LAST else 0
+            base = c0 if g == LAST else 0
             nc.vector.tensor_copy(picked[g, base][:, u, c0 - base : c1 - base], pairs[k][:].bitcast(U32).indirect(offs_sb[:, c0 // 16 : c1 // 16]))
 
         def new_input(g, h, tag):
@@ -102,7 +102,7 @@ def tile_attend_fill_kernel(tc, xT, w, cache, offs, slots, out):
         def weave(copy, g, c0, c1):
             h, first = c0 // HALF, c0 % HALF
             dst = x_bf[g, h][:].bitcast(U32).rearrange("p (n u) -> p n u", u=2)
-            base = c0 - c0 % HALF if g == LAST else 0
+            base = c0 if g == LAST else 0
             copy(dst[:, first : first + c1 - c0], picked[g, base][:].rearrange("p u n -> p n u")[:, c0 - base : c1 - base])
 
         def quant_x(g, c0, c1):
@@ -119,6 +119,11 @@ def tile_attend_fill_kernel(tc, xT, w, cache, offs, slots, out):
             dst = w_bf[g][:].rearrange("p (c i j) -> p c j i", i=4, j=PACK)
             src = w_raw[g][:].rearrange("p j (c i) -> p c j i", i=4)
             nc.scalar.activation(dst, src, COPY)
+
+        def cast_w_gpsimd(g, tag):
+            w_bf[g] = keep.tile([P, M * PACK], BF16, name="w_bf%d" % g, tag=tag, align_bytes=64)
+            dst = w_bf[g][:].rearrange("p (m j) -> p m j", j=PACK)
+            nc.gpsimd.tensor_copy(dst, w_raw[g][:].rearrange("p j m -> p m j"))
 
         def quant_w(g):
             nc.vector.quantize_mx(out=w_codes[g][:].bitcast(FP8X4), scales=w_scales[g][:], in_=w_bf[g][:])
@@ -148,37 +153,39 @@ def tile_attend_fill_kernel(tc, xT, w, cache, offs, slots, out):
         for k in range(PAIRS - 1):
             cast_x(k)
             if k // 2 == LAST:
-                gather(k, 0, HALF)
-                gather(k, HALF, G)
+                for c0, c1 in PIECES:
+                    gather(k, c0, c1)
             else:
                 gather(k, 0, G)
             if k >= 2:
                 g, h = divmod(k - 2, 2)
                 new_input(g, h, "raw%d" % k)
                 weave(nc.gpsimd.tensor_copy, g, h * HALF, (h + 1) * HALF)
-                new_codes(g, h, "x_codes%d_%d" % (g, h))
-                quant_x(g, h * HALF, (h + 1) * HALF)
+                if h == 0:
+                    new_codes(g, h, "x_codes%d_%d" % (g, h))
+                    quant_x(g, 0, HALF)
         cast_w_scalar(0, "w_bf0")
         quant_w(0)
         cast_x(PAIRS - 1)
-        new_input(1, 1, "raw5")
-        weave(nc.gpsimd.tensor_copy, 1, HALF, G)
         for c0, c1 in PIECES:
             gather(PAIRS - 1, c0, c1)
-        for g in range(1, PASSES):
-            cast_w_scalar(g, "w_bf%d" % g)
-            quant_w(g)
-        new_input(LAST, 0, "w_raw2")
-        new_codes(LAST, 0, "x_codes2_0")
+        cast_w_scalar(1, "w_bf1")
+        quant_w(1)
+        cast_w_gpsimd(LAST, "raw5")
+        quant_w(LAST)
+        new_input(LAST, 0, "w_raw1")
+        late_codes = keep.tile([P, 4 * HALF], U32, name="late_codes", tag="w_raw2", align_bytes=64)
+        for i, key in enumerate([(LAST, 0), (0, 1), (1, 1), (LAST, 1)]):
+            x_codes[key] = late_codes[:, i * HALF : (i + 1) * HALF]
         for c0, c1 in PIECES[:2]:
             weave(nc.scalar.copy, LAST, c0, c1)
             quant_x(LAST, c0, c1)
-        new_input(LAST, 1, "picked_last0")
+        new_input(1, 1, "picked_last0")
+        weave(nc.scalar.copy, 1, HALF, G)
+        new_input(LAST, 1, "picked_last128")
         weave(nc.scalar.copy, LAST, HALF, G)
-        new_codes(1, 1, "w_raw2")
-        quant_x(1, HALF, G)
-        new_codes(LAST, 1, "x_codes2_1")
-        quant_x(LAST, HALF, G)
+        for g in range(PASSES):
+            quant_x(g, HALF, G)
         for h in range(len(PIECES)):
             for g in range(PASSES):
                 multiply(g, h)

@@ -12,19 +12,22 @@ U16 = mybir.dt.uint16
 U8 = mybir.dt.uint8
 FP8X4 = mybir.dt.float8_e4m3fn_x4
 COPY = mybir.ActivationFunctionType.Copy
-MULT = mybir.AluOpType.mult
-ADD = mybir.AluOpType.add
 
 P = 128
 PACK = 4
 K_PASS = P * PACK
 PASSES = D // K_PASS
-PAIRS = 2 * PASSES
-HALF = G // 2
 LAST = PASSES - 1
-VECTOR_COLUMNS = [672, 672, 640, 288, 352, 400]
-EARLY = [0, 0, 0, 384, 384, 384]
-PIECES = [(0, 128), (128, 256), (256, 512)]
+PAIRS = 2 * PASSES
+PER_COLUMN = 16
+HALF = G // 2
+QUARTER = G // 4
+
+PIECES = [(0, QUARTER), (QUARTER, HALF), (HALF, G)]
+
+EARLY_COLUMNS = [0, 0, 0, 384, 384, 384]
+
+VECTOR_COLUMNS = [672, 672, 672, 288, 384, 448]
 
 
 def tile_attend_fill_kernel(tc, xT, w, cache, offs, slots, out):
@@ -33,21 +36,19 @@ def tile_attend_fill_kernel(tc, xT, w, cache, offs, slots, out):
         keep = ctx.enter_context(tc.tile_pool(name="keep", bufs=1))
         psum = ctx.enter_context(tc.psum_pool(name="psum", bufs=1))
 
-        offs_sb = keep.tile([P, G // 16], U16, name="offs_sb")
-        slots_sb = keep.tile([P, G // 16], U16, name="slots_sb")
+        offs_sb = keep.tile([P, G // PER_COLUMN], U16, name="offs_sb")
+        slots_sb = keep.tile([P, G // PER_COLUMN], U16, name="slots_sb")
         window = keep.tile([P, T2], F32, name="window")
         raw = [keep.tile([P, 2 * T], F32, name="raw%d" % k, align_bytes=64) for k in range(PAIRS)]
         pairs = [keep.tile([P, 2 * T], BF16, name="pairs%d" % k) for k in range(PAIRS)]
         picked = {(g, 0): keep.tile([P, 2, G], U32, name="picked%d" % g) for g in range(LAST)}
         for c0, c1 in PIECES:
-            picked.setdefault((LAST, c0), keep.tile([P, 2, c1 - c0], U32, name="picked_last%d" % c0, align_bytes=64))
+            picked[LAST, c0] = keep.tile([P, 2, c1 - c0], U32, name="picked_last%d" % c0, align_bytes=64)
         w_raw = [keep.tile([P, PACK, M], F32, name="w_raw%d" % g, align_bytes=64) for g in range(PASSES)]
         w_codes = [keep.tile([P, M], U32, name="w_codes%d" % g, align_bytes=64) for g in range(PASSES)]
         w_scales = [keep.tile([P, M], U8, name="w_scales%d" % g, align_bytes=64) for g in range(PASSES)]
         x_scales = [keep.tile([P, G], U8, name="x_scales%d" % g, align_bytes=64) for g in range(PASSES)]
         y = keep.tile([P, G], F32, name="y")
-        warm_in = keep.tile([P, 8], F32, name="warm_in")
-        warm_out = keep.tile([P, 8], F32, name="warm_out")
         acc = [psum.tile([P, c1 - c0], F32, name="acc%d" % c0) for c0, c1 in PIECES]
         x_bf = {}
         w_bf = {}
@@ -56,9 +57,9 @@ def tile_attend_fill_kernel(tc, xT, w, cache, offs, slots, out):
         def load_x(k):
             g, u = divmod(k, 2)
             rows = xT[g * K_PASS : (g + 1) * K_PASS, :].rearrange("(p u e) n -> p u (e n)", u=2, e=2)[:, u, :]
-            cut = T + EARLY[k] if EARLY[k] else 2 * T
+            cut = T + EARLY_COLUMNS[k] if EARLY_COLUMNS[k] else 2 * T
             nc.sync.dma_start(out=raw[k][:, :cut], in_=rows[:, :cut])
-            if EARLY[k]:
+            if EARLY_COLUMNS[k]:
                 nc.sync.dma_start(out=raw[k][:, cut:], in_=rows[:, cut:])
 
         def load_w(g):
@@ -76,120 +77,119 @@ def tile_attend_fill_kernel(tc, xT, w, cache, offs, slots, out):
         nc.sync.dma_start(slots_sb[:], slots)
         nc.sync.dma_start(out=window[:], in_=cache)
 
-        nc.gpsimd.memset(warm_in[:], 0.0)
-        nc.scalar.activation(warm_out[:], warm_in[:], COPY)
-
         def cast_x(k):
             src = raw[k][:].rearrange("p (e n) -> p n e", e=2)
             dst = pairs[k][:].rearrange("p (n e) -> p n e", e=2)
-            early, cut = EARLY[k], T - VECTOR_COLUMNS[k]
+            early, cut = EARLY_COLUMNS[k], T - VECTOR_COLUMNS[k]
             if early:
                 nc.scalar.activation(dst[:, :early, :], src[:, :early, :], COPY)
             nc.vector.tensor_copy(dst[:, cut:, :], src[:, cut:, :])
             nc.scalar.activation(dst[:, early:cut, :], src[:, early:cut, :], COPY)
 
-        def gather(k, c0, c1):
-            g, u = divmod(k, 2)
+        def picked_columns(g, c0, c1):
             base = c0 if g == LAST else 0
-            nc.vector.tensor_copy(picked[g, base][:, u, c0 - base : c1 - base], pairs[k][:].bitcast(U32).indirect(offs_sb[:, c0 // 16 : c1 // 16]))
+            return picked[g, base][:, :, c0 - base : c1 - base]
 
-        def new_input(g, h, tag):
-            x_bf[g, h] = keep.tile([P, HALF * PACK], BF16, name="x_bf%d_%d" % (g, h), tag=tag, align_bytes=64)
+        def gather(k):
+            g, u = divmod(k, 2)
+            for c0, c1 in PIECES if g == LAST else [(0, G)]:
+                entries = offs_sb[:, c0 // PER_COLUMN : c1 // PER_COLUMN]
+                nc.vector.tensor_copy(picked_columns(g, c0, c1)[:, u, :], pairs[k][:].bitcast(U32).indirect(entries))
 
-        def new_codes(g, h, tag):
-            x_codes[g, h] = keep.tile([P, HALF], U32, name="x_codes%d_%d" % (g, h), tag=tag, align_bytes=64)
+        def new_x_input(g, h, slot):
+            x_bf[g, h] = keep.tile([P, HALF * PACK], BF16, name="x_bf%d_%d" % (g, h), tag=slot, align_bytes=64)
+
+        def new_x_codes(name, slot, ranges):
+            width = sum(c1 - c0 for g, c0, c1 in ranges)
+            tile = keep.tile([P, width], U32, name=name, tag=slot, align_bytes=64)
+            at = 0
+            for g, c0, c1 in ranges:
+                x_codes[g, c0, c1] = tile[:, at : at + c1 - c0]
+                at = at + c1 - c0
 
         def weave(copy, g, c0, c1):
-            h, first = c0 // HALF, c0 % HALF
+            h, first = divmod(c0, HALF)
             dst = x_bf[g, h][:].bitcast(U32).rearrange("p (n u) -> p n u", u=2)
-            base = c0 if g == LAST else 0
-            copy(dst[:, first : first + c1 - c0], picked[g, base][:].rearrange("p u n -> p n u")[:, c0 - base : c1 - base])
+            copy(dst[:, first : first + c1 - c0], picked_columns(g, c0, c1).rearrange("p u n -> p n u"))
 
         def quant_x(g, c0, c1):
-            h, first = c0 // HALF, c0 % HALF
-            last = first + c1 - c0
+            h, first = divmod(c0, HALF)
             nc.vector.quantize_mx(
-                out=x_codes[g, h][:, first:last].bitcast(FP8X4),
+                out=x_codes[g, c0, c1].bitcast(FP8X4),
                 scales=x_scales[g][:, c0:c1],
-                in_=x_bf[g, h][:, PACK * first : PACK * last],
+                in_=x_bf[g, h][:, PACK * first : PACK * (first + c1 - c0)],
             )
 
-        def cast_w_scalar(g, tag):
-            w_bf[g] = keep.tile([P, M * PACK], BF16, name="w_bf%d" % g, tag=tag, align_bytes=64)
-            dst = w_bf[g][:].rearrange("p (c i j) -> p c j i", i=4, j=PACK)
-            src = w_raw[g][:].rearrange("p j (c i) -> p c j i", i=4)
-            nc.scalar.activation(dst, src, COPY)
+        def new_w_input(g, slot):
+            w_bf[g] = keep.tile([P, M * PACK], BF16, name="w_bf%d" % g, tag=slot, align_bytes=64)
 
-        def cast_w_gpsimd(g, tag):
-            w_bf[g] = keep.tile([P, M * PACK], BF16, name="w_bf%d" % g, tag=tag, align_bytes=64)
+        def cast_w_on_scalar(g):
+            dst = w_bf[g][:].rearrange("p (c i j) -> p c j i", i=4, j=PACK)
+            nc.scalar.activation(dst, w_raw[g][:].rearrange("p j (c i) -> p c j i", i=4), COPY)
+
+        def cast_w_on_gpsimd(g):
             dst = w_bf[g][:].rearrange("p (m j) -> p m j", j=PACK)
             nc.gpsimd.tensor_copy(dst, w_raw[g][:].rearrange("p j m -> p m j"))
 
         def quant_w(g):
             nc.vector.quantize_mx(out=w_codes[g][:].bitcast(FP8X4), scales=w_scales[g][:], in_=w_bf[g][:])
 
-        def multiply(g, h):
-            c0, c1 = PIECES[h]
-            first = c0 - c0 % HALF
+        def multiply(g, piece):
+            c0, c1 = PIECES[piece]
+            first, end = [(b0, b1) for gg, b0, b1 in x_codes if gg == g and b0 <= c0 < b1][0]
             nc.tensor.matmul_mx(
-                out=acc[h][:],
+                out=acc[piece][:],
                 lhsT=w_codes[g][:].bitcast(FP8X4),
                 lhsT_scale=w_scales[g][:],
-                rhs=x_codes[g, c0 // HALF][:, c0 - first : c1 - first].bitcast(FP8X4),
+                rhs=x_codes[g, first, end][:, c0 - first : c1 - first].bitcast(FP8X4),
                 rhs_scale=x_scales[g][:, c0:c1],
                 start=(g == 0),
                 stop=(g == LAST),
             )
 
-        def drain(h):
-            nc.scalar.copy(y[:, PIECES[h][0] : PIECES[h][1]], acc[h][:])
-
-        def scatter(h):
-            nc.vector.tensor_copy(
-                window[:].indirect(slots_sb[:, h * HALF // 16 : (h + 1) * HALF // 16]),
-                y[:, h * HALF : (h + 1) * HALF],
-            )
-
         for k in range(PAIRS - 1):
             cast_x(k)
-            if k // 2 == LAST:
-                for c0, c1 in PIECES:
-                    gather(k, c0, c1)
-            else:
-                gather(k, 0, G)
+            gather(k)
             if k >= 2:
                 g, h = divmod(k - 2, 2)
-                new_input(g, h, "raw%d" % k)
+                new_x_input(g, h, "raw%d" % k)
                 weave(nc.gpsimd.tensor_copy, g, h * HALF, (h + 1) * HALF)
                 if h == 0:
-                    new_codes(g, h, "x_codes%d_%d" % (g, h))
+                    new_x_codes("x_codes%d" % g, "x_codes%d" % g, [(g, 0, HALF)])
                     quant_x(g, 0, HALF)
-        cast_w_scalar(0, "w_bf0")
+        new_w_input(0, "w_bf0")
+        cast_w_on_scalar(0)
         quant_w(0)
+
         cast_x(PAIRS - 1)
-        for c0, c1 in PIECES:
-            gather(PAIRS - 1, c0, c1)
-        cast_w_scalar(1, "w_bf1")
+        gather(PAIRS - 1)
+        new_w_input(1, "w_bf1")
+        cast_w_on_scalar(1)
         quant_w(1)
-        cast_w_gpsimd(LAST, "raw5")
+        new_x_input(LAST, 0, "w_raw1")
+        new_x_codes("first_codes", "first_codes", [(LAST, 0, QUARTER)])
+        weave(nc.scalar.copy, LAST, 0, QUARTER)
+        quant_x(LAST, 0, QUARTER)
+        new_w_input(LAST, "raw%d" % (PAIRS - 1))
+        cast_w_on_gpsimd(LAST)
         quant_w(LAST)
-        new_input(LAST, 0, "w_raw1")
-        late_codes = keep.tile([P, 4 * HALF], U32, name="late_codes", tag="w_raw2", align_bytes=64)
-        for i, key in enumerate([(LAST, 0), (0, 1), (1, 1), (LAST, 1)]):
-            x_codes[key] = late_codes[:, i * HALF : (i + 1) * HALF]
-        for c0, c1 in PIECES[:2]:
-            weave(nc.scalar.copy, LAST, c0, c1)
-            quant_x(LAST, c0, c1)
-        new_input(1, 1, "picked_last0")
+        late = [(LAST, QUARTER, HALF)] + [(g, HALF, G) for g in range(PASSES)]
+        new_x_codes("late_codes", "w_raw%d" % LAST, late)
+        weave(nc.scalar.copy, LAST, QUARTER, HALF)
+        quant_x(LAST, QUARTER, HALF)
+
+        new_x_input(1, 1, "picked_last%d" % 0)
         weave(nc.scalar.copy, 1, HALF, G)
-        new_input(LAST, 1, "picked_last128")
+        new_x_input(LAST, 1, "picked_last%d" % QUARTER)
         weave(nc.scalar.copy, LAST, HALF, G)
         for g in range(PASSES):
             quant_x(g, HALF, G)
-        for h in range(len(PIECES)):
+
+        for piece, (c0, c1) in enumerate(PIECES):
             for g in range(PASSES):
-                multiply(g, h)
-            drain(h)
-        scatter(0)
-        scatter(1)
+                multiply(g, piece)
+            nc.scalar.copy(y[:, c0:c1], acc[piece][:])
+        for c0 in (0, HALF):
+            entries = slots_sb[:, c0 // PER_COLUMN : (c0 + HALF) // PER_COLUMN]
+            nc.vector.tensor_copy(window[:].indirect(entries), y[:, c0 : c0 + HALF])
         nc.sync.dma_start(out=out, in_=window[:])

@@ -41,9 +41,7 @@ def tile_attend_fill_kernel(tc, xT, w, cache, offs, slots, out):
         window = keep.tile([P, T2], F32, name="window")
         raw = [keep.tile([P, 2 * T], F32, name="raw%d" % k, align_bytes=64) for k in range(PAIRS)]
         pairs = [keep.tile([P, 2 * T], BF16, name="pairs%d" % k) for k in range(PAIRS)]
-        picked = {(g, 0): keep.tile([P, 2, G], U32, name="picked%d" % g) for g in range(LAST)}
-        for c0, c1 in PIECES:
-            picked[LAST, c0] = keep.tile([P, 2, c1 - c0], U32, name="picked_last%d" % c0, align_bytes=64)
+        picked = [keep.tile([P, 2, G], U32, name="picked%d" % g) for g in range(PASSES)]
         w_raw = [keep.tile([P, PACK, M], F32, name="w_raw%d" % g, align_bytes=64) for g in range(PASSES)]
         w_codes = [keep.tile([P, M], U32, name="w_codes%d" % g, align_bytes=64) for g in range(PASSES)]
         w_scales = [keep.tile([P, M], U8, name="w_scales%d" % g, align_bytes=64) for g in range(PASSES)]
@@ -86,18 +84,15 @@ def tile_attend_fill_kernel(tc, xT, w, cache, offs, slots, out):
             nc.vector.tensor_copy(dst[:, cut:, :], src[:, cut:, :])
             nc.scalar.activation(dst[:, early:cut, :], src[:, early:cut, :], COPY)
 
-        def picked_columns(g, c0, c1):
-            base = c0 if g == LAST else 0
-            return picked[g, base][:, :, c0 - base : c1 - base]
-
-        def gather(k):
+        def gather(k, c0, c1):
             g, u = divmod(k, 2)
-            for c0, c1 in PIECES if g == LAST else [(0, G)]:
-                entries = offs_sb[:, c0 // PER_COLUMN : c1 // PER_COLUMN]
-                nc.vector.tensor_copy(picked_columns(g, c0, c1)[:, u, :], pairs[k][:].bitcast(U32).indirect(entries))
+            entries = offs_sb[:, c0 // PER_COLUMN : c1 // PER_COLUMN]
+            nc.vector.tensor_copy(picked[g][:, u, c0:c1], pairs[k][:].bitcast(U32).indirect(entries))
 
-        def new_x_input(g, h, slot):
-            x_bf[g, h] = keep.tile([P, HALF * PACK], BF16, name="x_bf%d_%d" % (g, h), tag=slot, align_bytes=64)
+        def new_x_inputs(name, slot, halves):
+            tile = keep.tile([P, len(halves) * HALF * PACK], BF16, name=name, tag=slot, align_bytes=64)
+            for i, half in enumerate(halves):
+                x_bf[half] = tile[:, i * HALF * PACK : (i + 1) * HALF * PACK]
 
         def new_x_codes(name, slot, ranges):
             width = sum(c1 - c0 for g, c0, c1 in ranges)
@@ -109,8 +104,8 @@ def tile_attend_fill_kernel(tc, xT, w, cache, offs, slots, out):
 
         def weave(copy, g, c0, c1):
             h, first = divmod(c0, HALF)
-            dst = x_bf[g, h][:].bitcast(U32).rearrange("p (n u) -> p n u", u=2)
-            copy(dst[:, first : first + c1 - c0], picked_columns(g, c0, c1).rearrange("p u n -> p n u"))
+            dst = x_bf[g, h].bitcast(U32).rearrange("p (n u) -> p n u", u=2)
+            copy(dst[:, first : first + c1 - c0], picked[g][:].rearrange("p u n -> p n u")[:, c0:c1])
 
         def quant_x(g, c0, c1):
             h, first = divmod(c0, HALF)
@@ -149,10 +144,10 @@ def tile_attend_fill_kernel(tc, xT, w, cache, offs, slots, out):
 
         for k in range(PAIRS - 1):
             cast_x(k)
-            gather(k)
+            gather(k, 0, G)
             if k >= 2:
                 g, h = divmod(k - 2, 2)
-                new_x_input(g, h, "raw%d" % k)
+                new_x_inputs("x_bf%d_%d" % (g, h), "raw%d" % k, [(g, h)])
                 weave(nc.gpsimd.tensor_copy, g, h * HALF, (h + 1) * HALF)
                 if h == 0:
                     new_x_codes("x_codes%d" % g, "x_codes%d" % g, [(g, 0, HALF)])
@@ -162,11 +157,12 @@ def tile_attend_fill_kernel(tc, xT, w, cache, offs, slots, out):
         quant_w(0)
 
         cast_x(PAIRS - 1)
-        gather(PAIRS - 1)
+        for c0, c1 in PIECES:
+            gather(PAIRS - 1, c0, c1)
         new_w_input(1, "w_bf1")
         cast_w_on_scalar(1)
         quant_w(1)
-        new_x_input(LAST, 0, "w_raw1")
+        new_x_inputs("x_bf_late", "w_raw1", [(LAST, 0), (1, 1), (LAST, 1)])
         new_x_codes("first_codes", "first_codes", [(LAST, 0, QUARTER)])
         weave(nc.scalar.copy, LAST, 0, QUARTER)
         quant_x(LAST, 0, QUARTER)
@@ -178,10 +174,8 @@ def tile_attend_fill_kernel(tc, xT, w, cache, offs, slots, out):
         weave(nc.scalar.copy, LAST, QUARTER, HALF)
         quant_x(LAST, QUARTER, HALF)
 
-        new_x_input(1, 1, "picked_last%d" % 0)
-        weave(nc.scalar.copy, 1, HALF, G)
-        new_x_input(LAST, 1, "picked_last%d" % QUARTER)
-        weave(nc.scalar.copy, LAST, HALF, G)
+        for g in range(1, PASSES):
+            weave(nc.scalar.copy, g, HALF, G)
         for g in range(PASSES):
             quant_x(g, HALF, G)
 

@@ -11,6 +11,7 @@ U32 = mybir.dt.uint32
 U16 = mybir.dt.uint16
 U8 = mybir.dt.uint8
 FP8X4 = mybir.dt.float8_e4m3fn_x4
+ADD = mybir.AluOpType.add
 COPY = mybir.ActivationFunctionType.Copy
 
 P = 128
@@ -23,7 +24,8 @@ PER_COLUMN = 16
 HALF = G // 2
 QUARTER = G // 4
 
-PIECES = [(0, QUARTER), (QUARTER, HALF), (HALF, G)]
+PIECES = [(c0, c0 + QUARTER) for c0 in range(0, G, QUARTER)]
+GATHERS = [(0, QUARTER), (QUARTER, HALF), (HALF, G)]
 
 EARLY_COLUMNS = [0, 0, 0, 384, 384, 384]
 
@@ -47,6 +49,8 @@ def tile_attend_fill_kernel(tc, xT, w, cache, offs, slots, out):
         w_scales = [keep.tile([P, M], U8, name="w_scales%d" % g, align_bytes=64) for g in range(PASSES)]
         x_scales = [keep.tile([P, G], U8, name="x_scales%d" % g, align_bytes=64) for g in range(PASSES)]
         y = keep.tile([P, G], F32, name="y")
+        zeros = keep.tile([P, QUARTER], F32, name="zeros")
+        nc.gpsimd.memset(zeros[:], 0.0)
         acc = [psum.tile([P, c1 - c0], F32, name="acc%d" % c0) for c0, c1 in PIECES]
         x_bf = {}
         w_bf = {}
@@ -122,6 +126,10 @@ def tile_attend_fill_kernel(tc, xT, w, cache, offs, slots, out):
             dst = w_bf[g][:].rearrange("p (c i j) -> p c j i", i=4, j=PACK)
             nc.scalar.activation(dst, w_raw[g][:].rearrange("p j (c i) -> p c j i", i=4), COPY)
 
+        def cast_w_on_vector(g):
+            dst = w_bf[g][:].rearrange("p (c i j) -> p c j i", i=4, j=PACK)
+            nc.vector.tensor_copy(dst, w_raw[g][:].rearrange("p j (c i) -> p c j i", i=4))
+
         def cast_w_on_gpsimd(g):
             dst = w_bf[g][:].rearrange("p (m j) -> p m j", j=PACK)
             nc.gpsimd.tensor_copy(dst, w_raw[g][:].rearrange("p j m -> p m j"))
@@ -144,6 +152,9 @@ def tile_attend_fill_kernel(tc, xT, w, cache, offs, slots, out):
 
         for k in range(PAIRS - 1):
             cast_x(k)
+            if k == PAIRS - 2:
+                new_w_input(0, "w_bf0")
+                cast_w_on_vector(0)
             gather(k, 0, G)
             if k >= 2:
                 g, h = divmod(k - 2, 2)
@@ -152,38 +163,39 @@ def tile_attend_fill_kernel(tc, xT, w, cache, offs, slots, out):
                 if h == 0:
                     new_x_codes("x_codes%d" % g, "x_codes%d" % g, [(g, 0, HALF)])
                     quant_x(g, 0, HALF)
-        new_w_input(0, "w_bf0")
-        cast_w_on_scalar(0)
         quant_w(0)
+        new_x_inputs("x_bf1_1", "w_raw0", [(1, 1)])
+        weave(nc.scalar.copy, 1, HALF, G)
 
         cast_x(PAIRS - 1)
-        for c0, c1 in PIECES:
+        for c0, c1 in GATHERS:
             gather(PAIRS - 1, c0, c1)
         new_w_input(1, "w_bf1")
         cast_w_on_scalar(1)
         quant_w(1)
-        new_x_inputs("x_bf_late", "w_raw1", [(LAST, 0), (1, 1), (LAST, 1)])
+        new_x_inputs("x_bf_late", "w_raw1", [(LAST, 0), (LAST, 1)])
         new_x_codes("first_codes", "first_codes", [(LAST, 0, QUARTER)])
         weave(nc.scalar.copy, LAST, 0, QUARTER)
         quant_x(LAST, 0, QUARTER)
         new_w_input(LAST, "raw%d" % (PAIRS - 1))
         cast_w_on_gpsimd(LAST)
         quant_w(LAST)
-        late = [(LAST, QUARTER, HALF)] + [(g, HALF, G) for g in range(PASSES)]
+        late = [(LAST, QUARTER, HALF)] + [(g, HALF, G) for g in range(LAST)] + [(LAST, c0, c1) for c0, c1 in PIECES[2:]]
         new_x_codes("late_codes", "w_raw%d" % LAST, late)
         weave(nc.scalar.copy, LAST, QUARTER, HALF)
         quant_x(LAST, QUARTER, HALF)
 
-        for g in range(1, PASSES):
-            weave(nc.scalar.copy, g, HALF, G)
-        for g in range(PASSES):
+        for g in range(LAST):
             quant_x(g, HALF, G)
+        for c0, c1 in PIECES[2:]:
+            weave(nc.scalar.copy, LAST, c0, c1)
+            quant_x(LAST, c0, c1)
 
         for piece, (c0, c1) in enumerate(PIECES):
             for g in range(PASSES):
                 multiply(g, piece)
             nc.scalar.copy(y[:, c0:c1], acc[piece][:])
-        for c0 in (0, HALF):
-            entries = slots_sb[:, c0 // PER_COLUMN : (c0 + HALF) // PER_COLUMN]
-            nc.vector.tensor_copy(window[:].indirect(entries), y[:, c0 : c0 + HALF])
+        first = QUARTER // PER_COLUMN
+        nc.vector.tensor_tensor(window[:].indirect(slots_sb[:, :first]), y[:, :QUARTER], zeros[:], ADD)
+        nc.vector.tensor_copy(window[:].indirect(slots_sb[:, first:]), y[:, QUARTER:])
         nc.sync.dma_start(out=out, in_=window[:])

@@ -25,7 +25,7 @@ HALF = G // 2
 QUARTER = G // 4
 
 PIECES = [(c0, c0 + QUARTER) for c0 in range(0, G, QUARTER)]
-GATHERS = [(0, QUARTER), (QUARTER, HALF), (HALF, G)]
+GATHERS = [(0, QUARTER), (QUARTER, G)]
 
 EARLY_COLUMNS = [0, 0, 0, 384, 384, 384]
 
@@ -182,12 +182,10 @@ def tile_attend_fill_kernel(tc, xT, w, cache, offs, slots, out):
         quant_w(LAST)
         late = [(LAST, QUARTER, HALF)] + [(g, HALF, G) for g in range(LAST)] + [(LAST, c0, c1) for c0, c1 in PIECES[2:]]
         new_x_codes("late_codes", "w_raw%d" % LAST, late)
-        weave(nc.scalar.copy, LAST, QUARTER, HALF)
-        quant_x(LAST, QUARTER, HALF)
 
         for g in range(LAST):
             quant_x(g, HALF, G)
-        for c0, c1 in PIECES[2:]:
+        for c0, c1 in PIECES[1:]:
             weave(nc.scalar.copy, LAST, c0, c1)
             quant_x(LAST, c0, c1)
 

from contextlib import ExitStack

import concourse.mybir as mybir

G, T, T2, D, M = 512, 1024, 2048, 1536, 128
FLOPS = 2 * D * M * G

F32 = mybir.dt.float32
BF16 = mybir.dt.bfloat16
U32 = mybir.dt.uint32
U16 = mybir.dt.uint16
U8 = mybir.dt.uint8
FP8X4 = mybir.dt.float8_e4m3fn_x4
ADD = mybir.AluOpType.add
COPY = mybir.ActivationFunctionType.Copy

P = 128
PACK = 4
K_PASS = P * PACK
PASSES = D // K_PASS
LAST = PASSES - 1
PAIRS = 2 * PASSES
PER_COLUMN = 16
HALF = G // 2
QUARTER = G // 4

PIECES = [(c0, c0 + QUARTER) for c0 in range(0, G, QUARTER)]
GATHERS = [(0, QUARTER), (QUARTER, G)]

EARLY_COLUMNS = [0, 0, 0, 384, 384, 384]

VECTOR_COLUMNS = [672, 672, 672, 288, 384, 448]


def tile_attend_fill_kernel(tc, xT, w, cache, offs, slots, out):
    nc = tc.nc
    with ExitStack() as ctx:
        keep = ctx.enter_context(tc.tile_pool(name="keep", bufs=1))
        psum = ctx.enter_context(tc.psum_pool(name="psum", bufs=1))

        offs_sb = keep.tile([P, G // PER_COLUMN], U16, name="offs_sb")
        slots_sb = keep.tile([P, G // PER_COLUMN], U16, name="slots_sb")
        window = keep.tile([P, T2], F32, name="window")
        raw = [keep.tile([P, 2 * T], F32, name="raw%d" % k, align_bytes=64) for k in range(PAIRS)]
        pairs = [keep.tile([P, 2 * T], BF16, name="pairs%d" % k) for k in range(PAIRS)]
        picked = [keep.tile([P, 2, G], U32, name="picked%d" % g) for g in range(PASSES)]
        w_raw = [keep.tile([P, PACK, M], F32, name="w_raw%d" % g, align_bytes=64) for g in range(PASSES)]
        w_codes = [keep.tile([P, M], U32, name="w_codes%d" % g, align_bytes=64) for g in range(PASSES)]
        w_scales = [keep.tile([P, M], U8, name="w_scales%d" % g, align_bytes=64) for g in range(PASSES)]
        x_scales = [keep.tile([P, G], U8, name="x_scales%d" % g, align_bytes=64) for g in range(PASSES)]
        y = keep.tile([P, G], F32, name="y")
        zeros = keep.tile([P, QUARTER], F32, name="zeros")
        nc.gpsimd.memset(zeros[:], 0.0)
        acc = [psum.tile([P, c1 - c0], F32, name="acc%d" % c0) for c0, c1 in PIECES]
        x_bf = {}
        w_bf = {}
        x_codes = {}

        def load_x(k):
            g, u = divmod(k, 2)
            rows = xT[g * K_PASS : (g + 1) * K_PASS, :].rearrange("(p u e) n -> p u (e n)", u=2, e=2)[:, u, :]
            cut = T + EARLY_COLUMNS[k] if EARLY_COLUMNS[k] else 2 * T
            nc.sync.dma_start(out=raw[k][:, :cut], in_=rows[:, :cut])
            if EARLY_COLUMNS[k]:
                nc.sync.dma_start(out=raw[k][:, cut:], in_=rows[:, cut:])

        def load_w(g):
            rows = w[g * K_PASS : (g + 1) * K_PASS, :].rearrange("(p j) m -> p j m", j=PACK)
            nc.sync.dma_start(out=w_raw[g][:], in_=rows)

        load_x(0)
        nc.sync.dma_start(offs_sb[:], offs)
        for k in range(1, PAIRS - 1):
            load_x(k)
        load_w(0)
        load_x(PAIRS - 1)
        for g in range(1, PASSES):
            load_w(g)
        nc.sync.dma_start(slots_sb[:], slots)
        nc.sync.dma_start(out=window[:], in_=cache)

        def cast_x(k):
            src = raw[k][:].rearrange("p (e n) -> p n e", e=2)
            dst = pairs[k][:].rearrange("p (n e) -> p n e", e=2)
            early, cut = EARLY_COLUMNS[k], T - VECTOR_COLUMNS[k]
            if early:
                nc.scalar.activation(dst[:, :early, :], src[:, :early, :], COPY)
            nc.vector.tensor_copy(dst[:, cut:, :], src[:, cut:, :])
            nc.scalar.activation(dst[:, early:cut, :], src[:, early:cut, :], COPY)

        def gather(k, c0, c1):
            g, u = divmod(k, 2)
            entries = offs_sb[:, c0 // PER_COLUMN : c1 // PER_COLUMN]
            nc.vector.tensor_copy(picked[g][:, u, c0:c1], pairs[k][:].bitcast(U32).indirect(entries))

        def new_x_inputs(name, slot, halves):
            tile = keep.tile([P, len(halves) * HALF * PACK], BF16, name=name, tag=slot, align_bytes=64)
            for i, half in enumerate(halves):
                x_bf[half] = tile[:, i * HALF * PACK : (i + 1) * HALF * PACK]

        def new_x_codes(name, slot, ranges):
            width = sum(c1 - c0 for g, c0, c1 in ranges)
            tile = keep.tile([P, width], U32, name=name, tag=slot, align_bytes=64)
            at = 0
            for g, c0, c1 in ranges:
                x_codes[g, c0, c1] = tile[:, at : at + c1 - c0]
                at = at + c1 - c0

        def weave(copy, g, c0, c1):
            h, first = divmod(c0, HALF)
            dst = x_bf[g, h].bitcast(U32).rearrange("p (n u) -> p n u", u=2)
            copy(dst[:, first : first + c1 - c0], picked[g][:].rearrange("p u n -> p n u")[:, c0:c1])

        def quant_x(g, c0, c1):
            h, first = divmod(c0, HALF)
            nc.vector.quantize_mx(
                out=x_codes[g, c0, c1].bitcast(FP8X4),
                scales=x_scales[g][:, c0:c1],
                in_=x_bf[g, h][:, PACK * first : PACK * (first + c1 - c0)],
            )

        def new_w_input(g, slot):
            w_bf[g] = keep.tile([P, M * PACK], BF16, name="w_bf%d" % g, tag=slot, align_bytes=64)

        def cast_w_on_scalar(g):
            dst = w_bf[g][:].rearrange("p (c i j) -> p c j i", i=4, j=PACK)
            nc.scalar.activation(dst, w_raw[g][:].rearrange("p j (c i) -> p c j i", i=4), COPY)

        def cast_w_on_vector(g):
            dst = w_bf[g][:].rearrange("p (c i j) -> p c j i", i=4, j=PACK)
            nc.vector.tensor_copy(dst, w_raw[g][:].rearrange("p j (c i) -> p c j i", i=4))

        def cast_w_on_gpsimd(g):
            dst = w_bf[g][:].rearrange("p (m j) -> p m j", j=PACK)
            nc.gpsimd.tensor_copy(dst, w_raw[g][:].rearrange("p j m -> p m j"))

        def quant_w(g):
            nc.vector.quantize_mx(out=w_codes[g][:].bitcast(FP8X4), scales=w_scales[g][:], in_=w_bf[g][:])

        def multiply(g, piece):
            c0, c1 = PIECES[piece]
            first, end = [(b0, b1) for gg, b0, b1 in x_codes if gg == g and b0 <= c0 < b1][0]
            nc.tensor.matmul_mx(
                out=acc[piece][:],
                lhsT=w_codes[g][:].bitcast(FP8X4),
                lhsT_scale=w_scales[g][:],
                rhs=x_codes[g, first, end][:, c0 - first : c1 - first].bitcast(FP8X4),
                rhs_scale=x_scales[g][:, c0:c1],
                start=(g == 0),
                stop=(g == LAST),
            )

        for k in range(PAIRS - 1):
            cast_x(k)
            if k == PAIRS - 2:
                new_w_input(0, "w_bf0")
                cast_w_on_vector(0)
            gather(k, 0, G)
            if k >= 2:
                g, h = divmod(k - 2, 2)
                new_x_inputs("x_bf%d_%d" % (g, h), "raw%d" % k, [(g, h)])
                weave(nc.gpsimd.tensor_copy, g, h * HALF, (h + 1) * HALF)
                if h == 0:
                    new_x_codes("x_codes%d" % g, "x_codes%d" % g, [(g, 0, HALF)])
                    quant_x(g, 0, HALF)
        quant_w(0)
        new_x_inputs("x_bf1_1", "w_raw0", [(1, 1)])
        weave(nc.scalar.copy, 1, HALF, G)

        cast_x(PAIRS - 1)
        for c0, c1 in GATHERS:
            gather(PAIRS - 1, c0, c1)
        new_w_input(1, "w_bf1")
        cast_w_on_scalar(1)
        quant_w(1)
        new_x_inputs("x_bf_late", "w_raw1", [(LAST, 0), (LAST, 1)])
        new_x_codes("first_codes", "first_codes", [(LAST, 0, QUARTER)])
        weave(nc.scalar.copy, LAST, 0, QUARTER)
        quant_x(LAST, 0, QUARTER)
        new_w_input(LAST, "raw%d" % (PAIRS - 1))
        cast_w_on_gpsimd(LAST)
        quant_w(LAST)
        late = [(LAST, QUARTER, HALF)] + [(g, HALF, G) for g in range(LAST)] + [(LAST, c0, c1) for c0, c1 in PIECES[2:]]
        new_x_codes("late_codes", "w_raw%d" % LAST, late)

        for g in range(LAST):
            quant_x(g, HALF, G)
        for c0, c1 in PIECES[1:]:
            weave(nc.scalar.copy, LAST, c0, c1)
            quant_x(LAST, c0, c1)

        for piece, (c0, c1) in enumerate(PIECES):
            for g in range(PASSES):
                multiply(g, piece)
            nc.scalar.copy(y[:, c0:c1], acc[piece][:])
        first = QUARTER // PER_COLUMN
        nc.vector.tensor_tensor(window[:].indirect(slots_sb[:, :first]), y[:, :QUARTER], zeros[:], ADD)
        nc.vector.tensor_copy(window[:].indirect(slots_sb[:, first:]), y[:, QUARTER:])
        nc.sync.dma_start(out=out, in_=window[:])
